import numpy as np
import ml_dtypes


def mxq(x, axis, fmt="e4m3"):
    dtype, down = {"e4m3": (ml_dtypes.float8_e4m3fn, 7), "e5m2": (ml_dtypes.float8_e5m2, 14)}[fmt]
    v = np.moveaxis(np.asarray(x, np.float32).astype(ml_dtypes.bfloat16).astype(np.float64), axis, -1)
    blocks = v.reshape(v.shape[:-1] + (-1, 32))
    amax = np.abs(blocks).max(-1, keepdims=True)
    byte = np.maximum(np.where(amax > 0, np.frexp(amax)[1] - 1 + 127, 0) - down, 1)
    scale = np.exp2(byte - 127.0)
    codes = (blocks / scale).astype(np.float32).astype(dtype).astype(np.float64)
    return np.moveaxis((codes * scale).reshape(v.shape), -1, axis)


WIDE = False


def mx_kscale(k):
    if not WIDE:
        return np.ones(k)
    levels = np.array([10, -10, 5, -5, 0])
    if k % 512:
        return np.exp2(np.random.permutation(np.resize(levels, k // 32))).repeat(32)
    a = np.empty((k // 512, 16))
    for p in range(k // 512):
        a[p, :8] = np.random.permutation(np.resize(levels, 8))
        for g in range(8):
            far = levels[np.abs(levels - a[p, g]) >= 10]
            a[p, g + 8] = far[np.random.randint(len(far))]
    return np.exp2(a.ravel()).repeat(32)


def f64(x):
    return np.asarray(x).astype(np.float64)


def striped(idx):
    return np.tile(idx.reshape(-1, 16).T, (8, 1)).astype(np.uint16)


def unstriped(offs):
    return offs[:16].T.reshape(-1).astype(np.int64)


def striped8(idx):
    return np.concatenate([x.reshape(-1, 16).T for x in idx]).astype(np.uint16)


def runs(offs, k):
    lists = np.stack([offs[16 * r : 16 * r + 16].T.reshape(-1) for r in range(8)]).astype(np.int64)
    return lists[np.arange(k) % 512 // 64]


def pack_weight(w):
    k, n = w.shape
    w = f64(np.asarray(w, np.float32).astype(ml_dtypes.bfloat16)).reshape(k // 32, 32, n)
    amax = np.abs(w).max(1)
    byte = np.clip(np.where(amax > 0, np.frexp(amax)[1] - 1 + 127 - 7, 1), 1, 254)
    scaled = (w * np.exp2(127.0 - byte)[:, None, :]).reshape(k, n).astype(np.float32)
    words = np.ascontiguousarray(scaled.reshape(k // 512, 128, 4, n).transpose(0, 1, 3, 2)).astype(ml_dtypes.float8_e4m3fn).view(np.uint8)
    return words, np.ascontiguousarray(byte.astype(np.uint8).reshape(k // 512, 16, n))


def unpack_weight(words, scales):
    g, p, n, _ = words.shape
    vals = np.ascontiguousarray(words).view(ml_dtypes.float8_e4m3fn).astype(np.float64) * np.repeat(np.exp2(scales.astype(np.float64) - 127.0), 8, axis=1)[..., None]
    return vals.transpose(0, 1, 3, 2).reshape(g * 512, n)


K, T, S, N, G, H, J = 512, 1024, 256, 512, 2048, 512, 512


def setup_inputs():
    n = np.random.standard_normal
    s = mx_kscale(K)[:, None]
    u = mx_kscale(K)
    packed_xT = pack_weight(n((K, T)) * s)
    packed_dT = pack_weight(n((K, G)) / s)
    return {
        "x_words": packed_xT[0],
        "x_scales": packed_xT[1],
        "d_words": packed_dT[0],
        "d_scales": packed_dT[1],
        "tab": n((H, J)).astype(np.float32),
        "gn": (np.random.uniform(0.5, 1.5, (H, 1)) * u[:, None]).astype(np.float32),
        "gm": (np.random.uniform(0.5, 1.5, (H, 1)) * u[:, None]).astype(np.float32),
        "w1": (n((H, N)) / np.sqrt(2 * H) / u[:, None]).astype(np.float32),
        "w2": (n((H, N)) / np.sqrt(2 * H) / u[:, None]).astype(np.float32),
        "offs": striped(np.random.permutation(T)[:S]),
        "k1": striped8(np.random.randint(0, G, (8, H))),
        "two": striped(np.random.permutation(T)[:S]),
        "k2": striped8(np.random.randint(0, G, (8, H))),
        "n1": striped(np.random.permutation(S)),
        "n2": striped(np.random.permutation(S)),
        "n3": striped(np.random.randint(0, J, S)),
        "n4": striped(np.random.randint(0, J, S)),
        "n5": striped(np.random.permutation(S)),
        "n6": striped(np.random.permutation(S)),
        "n7": striped(np.random.permutation(S)),
    }


def reference(x_words, x_scales, d_words, d_scales, tab, gn, gm, w1, w2, offs, k1, two, k2, n1, n2, n3, n4, n5, n6, n7):
    d_k1 = unpack_weight(d_words, d_scales)[np.arange(K)[:, None], runs(k1, K)]
    xq = unpack_weight(x_words, x_scales)[:, unstriped(offs)]
    a = 0.0625 * (d_k1.T @ xq)
    z = f64(gn) * (a[:, unstriped(n1)] - a[:, unstriped(n2)])
    d_k2 = unpack_weight(d_words, d_scales)[np.arange(K)[:, None], runs(k2, K)]
    x_two = unpack_weight(x_words, x_scales)[:, unstriped(two)]
    b = 0.0625 * (d_k2.T @ x_two)
    z2 = f64(gm) * (b[:, unstriped(n5)] * f64(tab)[:, unstriped(n3)] + f64(tab)[:, unstriped(n4)])
    h = mxq(f64(w1), 0, "e4m3").T @ mxq(z, 0, "e4m3") + mxq(f64(w2), 0, "e4m3").T @ mxq(z2, 0, "e4m3")
    st = np.maximum(h, h[:, unstriped(n6)])
    return st[:, unstriped(n7)] - (0.5 * h)

@@ -1,0 +1,229 @@
+from contextlib import ExitStack
+
+import concourse.mybir as mybir
+
+K, T, S, N, G, H, J = 512, 1024, 256, 512, 2048, 512, 512
+FLOPS = 2 * (2 * K * H * S) + 2 * (2 * H * N * S)
+
+F32 = mybir.dt.float32
+BF16 = mybir.dt.bfloat16
+I32 = mybir.dt.int32
+U32 = mybir.dt.uint32
+U16 = mybir.dt.uint16
+U8 = mybir.dt.uint8
+FP8X4 = mybir.dt.float8_e4m3fn_x4
+ALU = mybir.AluOpType
+COPY = mybir.ActivationFunctionType.Copy
+
+P = 128
+PACK = 4
+SPARE = 8
+LIST_ROWS = 16
+
+
+def tile_picked_pqjgapkindahopb_none_p_kernel(
+    tc, x_words, x_scales, d_words, d_scales, tab, gn, gm, w1, w2, offs, k1, two, k2, n1, n2, n3, n4, n5, n6, n7, out
+):
+    nc = tc.nc
+    with ExitStack() as ctx:
+        keep = ctx.enter_context(tc.tile_pool(name="keep", bufs=1))
+        psum = ctx.enter_context(tc.psum_pool(name="psum", bufs=1))
+
+        def load_list(name, src):
+            tile = keep.tile(list(src.shape), U16, name="list_" + name)
+            nc.sync.dma_start(tile[:], src)
+            return tile
+
+        def result_window(name):
+            tile = keep.tile([P, S + SPARE], F32, name=name)
+            nc.gpsimd.memset(tile[:, S:], 0.0)
+            return tile
+
+        def fetch(dst, window, places, lo=0, hi=S):
+            nc.scalar.activation(dst[:, lo:hi], window[:].indirect(places[:, lo // LIST_ROWS : hi // LIST_ROWS]), COPY)
+
+        d_byte_table = keep.tile([P, G], U8)
+        x_byte_table = keep.tile([P, T], U8)
+        planes = keep.tile([P, 2 * (H + S)], U8, align_bytes=64)
+        nc.vector.memset(d_byte_table[:].bitcast(I32), 0)
+        nc.vector.memset(x_byte_table[:].bitcast(I32), 0)
+        nc.gpsimd.memset(planes[:].bitcast(I32), 0)
+
+        k2_list = load_list("k2", k2)
+        k1_list = load_list("k1", k1)
+        two_list = load_list("two", two)
+        nc.sync.dma_start(d_byte_table[0:P:8, :].bitcast(I32), d_scales[0].bitcast(I32))
+        nc.sync.dma_start(x_byte_table[0:P:8, :].bitcast(I32), x_scales[0].bitcast(I32))
+        offs_list = load_list("offs", offs)
+
+        tab_rows = tab.rearrange("(p t) c -> p t c", t=PACK)
+        tab_tiles = [keep.tile([P, J], F32, name="tab%d" % t) for t in range(PACK)]
+        x_word_table = keep.tile([P, T], U32)
+        d_word_table = keep.tile([P, G], U32)
+        nc.sync.dma_start(tab_tiles[0][:], tab_rows[:, 0, :])
+        nc.sync.dma_start(x_word_table[:].bitcast(I32), x_words[0].rearrange("p n t -> p (n t)").bitcast(I32))
+        n3_list = load_list("n3", n3)
+        n4_list = load_list("n4", n4)
+        nc.sync.dma_start(d_word_table[:].bitcast(I32), d_words[0].rearrange("p n t -> p (n t)").bitcast(I32))
+        nc.sync.dma_start(tab_tiles[1][:], tab_rows[:, 1, :])
+        gm_cols = keep.tile([P, PACK], F32)
+        gn_cols = keep.tile([P, PACK], F32)
+        nc.sync.dma_start(gm_cols[:], gm.rearrange("(p t) o -> p (t o)", t=PACK))
+        nc.sync.dma_start(gn_cols[:], gn.rearrange("(p t) o -> p (t o)", t=PACK))
+        nc.sync.dma_start(tab_tiles[2][:], tab_rows[:, 2, :])
+        nc.sync.dma_start(tab_tiles[3][:], tab_rows[:, 3, :])
+        n5_list = load_list("n5", n5)
+        n1_list = load_list("n1", n1)
+        n2_list = load_list("n2", n2)
+
+        staged = keep.tile([P, 2 * (H + S)], U8)
+        x_bytes = keep.tile([P, 2 * S], U8)
+        for s, codes in enumerate((k2_list, k1_list)):
+            d_bytes = keep.tile([P, H], U8, name="d_bytes%d" % s)
+            nc.vector.tensor_copy(d_bytes[:], d_byte_table[:].indirect(codes[:]))
+            nc.vector.tensor_copy(
+                staged[:, s * H : (s + 1) * H].rearrange("p (t c i) -> p c t i", t=PACK, i=16),
+                d_bytes[:].rearrange("p (c i t) -> p c t i", t=PACK, i=16),
+            )
+        for s, tokens in enumerate((two_list, offs_list)):
+            nc.vector.tensor_copy(x_bytes[:, s * S : (s + 1) * S], x_byte_table[:].indirect(tokens[:]))
+        nc.vector.tensor_copy(staged[:, 2 * H :], x_bytes[:])
+        for q in range(4):
+            nc.scalar.dma_start(
+                planes[32 * q : 32 * q + 4, :].bitcast(I32), staged[32 * q : 32 * q + 32 : 8, :].bitcast(I32)
+            )
+
+        w_raw = []
+        for s, w in enumerate((w2, w1)):
+            raw = keep.tile([P, PACK, N], F32, name="w_raw%d" % s)
+            nc.sync.dma_start(raw[:], w.rearrange("(p t) n -> p t n", t=PACK))
+            w_raw.append(raw)
+        n6_list = load_list("n6", n6)
+        n7_list = load_list("n7", n7)
+
+        gm_16th = keep.tile([P, PACK], F32)
+        gn_16th = keep.tile([P, PACK], F32)
+        nc.gpsimd.tensor_scalar(gm_16th[:], gm_cols[:], 0.0625, 0.0, ALU.mult, ALU.add)
+        nc.gpsimd.tensor_scalar(gn_16th[:], gn_cols[:], 0.0625, 0.0, ALU.mult, ALU.add)
+
+        tab_n3 = keep.tile([P, PACK, S], F32)
+        tab_n4 = keep.tile([P, PACK, S], F32)
+        shift = keep.tile([P, PACK, S], F32)
+        for t in range(PACK):
+            fetch(tab_n4[:, t, :], tab_tiles[t], n4_list)
+            fetch(tab_n3[:, t, :], tab_tiles[t], n3_list)
+            nc.gpsimd.tensor_scalar(shift[:, t, :], tab_n4[:, t, :], gm_cols[:, t : t + 1], 0.0, ALU.mult, ALU.add)
+
+        def coded_product(s, codes, tokens):
+            x_picked = keep.tile([P, S], U32, name="x_picked%d" % s, align_bytes=64)
+            d_picked = keep.tile([P, H], U32, name="d_picked%d" % s)
+            d_dealt = keep.tile([P, H], U32, name="d_dealt%d" % s, align_bytes=64)
+            nc.vector.tensor_copy(x_picked[:], x_word_table[:].indirect(tokens[:]))
+            nc.vector.tensor_copy(d_picked[:], d_word_table[:].indirect(codes[:]))
+            nc.vector.tensor_copy(
+                d_dealt[:].bitcast(I32).rearrange("p (t c i) -> p c t i", t=PACK, i=4),
+                d_picked[:].bitcast(I32).rearrange("p (c i t) -> p c t i", t=PACK, i=4),
+            )
+            banks = []
+            for t in range(PACK):
+                bank = psum.tile([P, S], F32, name="bank%d" % (PACK * s + t))
+                nc.tensor.matmul_mx(
+                    bank[:],
+                    lhsT=d_dealt[:, t * P : (t + 1) * P].bitcast(FP8X4),
+                    lhsT_scale=planes[:, s * H + t * P : s * H + (t + 1) * P],
+                    rhs=x_picked[:].bitcast(FP8X4),
+                    rhs_scale=planes[:, 2 * H + s * S : 2 * H + (s + 1) * S],
+                    start=True,
+                    stop=True,
+                )
+                banks.append(bank)
+            return banks
+
+        def woven(planar, lo, hi):
+            return planar[:, :, lo:hi].rearrange("p t (c i) -> p c t i", i=4)
+
+        def weave_target(grouped, lo, hi):
+            return grouped[:, lo:hi, :].rearrange("p (c i) t -> p c t i", i=4)
+
+        def quantize(codes, scales, grouped, lo, hi):
+            nc.vector.quantize_mx(
+                codes[:, lo:hi].bitcast(FP8X4), scales[:, lo:hi], grouped[:, lo:hi, :].rearrange("p c t -> p (c t)")
+            )
+
+        b_banks = coded_product(0, k2_list, two_list)
+        a_banks = coded_product(1, k1_list, offs_list)
+        b_n5 = keep.tile([P, PACK, S], F32)
+        for t in range(PACK):
+            b_window = result_window("b%d" % t)
+            nc.scalar.activation(b_window[:, :S], b_banks[t][:], COPY, scale=gm_16th[:, t : t + 1])
+            fetch(b_n5[:, t, :], b_window, n5_list)
+
+        a_windows = []
+        for t in range(PACK):
+            a_window = result_window("a%d" % t)
+            nc.vector.tensor_scalar(a_window[:, :S], a_banks[t][:], gn_16th[:, t : t + 1], None, ALU.mult)
+            a_windows.append(a_window)
+
+        w_codes, w_scales = [], []
+        for s in range(2):
+            grouped = keep.tile([P, N, PACK], BF16, name="w_grouped%d" % s, align_bytes=64)
+            codes = keep.tile([P, N], U32, name="w_codes%d" % s, align_bytes=64)
+            scales = keep.tile([P, N], U8, name="w_scales%d" % s, align_bytes=64)
+            nc.vector.tensor_copy(weave_target(grouped, 0, N), woven(w_raw[s], 0, N))
+            quantize(codes, scales, grouped, 0, N)
+            w_codes.append(codes)
+            w_scales.append(scales)
+
+        scaled = keep.tile([P, PACK, S], F32)
+        z2_grouped = keep.tile([P, S, PACK], BF16, align_bytes=64)
+        z2_codes = keep.tile([P, S], U32, align_bytes=64)
+        z2_scales = keep.tile([P, S], U8, align_bytes=64)
+        nc.vector.tensor_tensor(scaled[:], b_n5[:], tab_n3[:], ALU.mult)
+        nc.vector.tensor_tensor(weave_target(z2_grouped, 0, S), woven(scaled, 0, S), woven(shift, 0, S), ALU.add)
+        quantize(z2_codes, z2_scales, z2_grouped, 0, S)
+
+        a_n1 = keep.tile([P, PACK, S], F32)
+        a_n2 = keep.tile([P, PACK, S], F32)
+        z_grouped = keep.tile([P, S, PACK], BF16, align_bytes=64)
+        z_codes = keep.tile([P, S], U32, align_bytes=64)
+        z_scales = keep.tile([P, S], U8, align_bytes=64)
+        for lo, hi in ((0, S // 2), (S // 2, S)):
+            for t in range(PACK):
+                fetch(a_n1[:, t, :], a_windows[t], n1_list, lo, hi)
+                fetch(a_n2[:, t, :], a_windows[t], n2_list, lo, hi)
+            nc.vector.tensor_tensor(
+                weave_target(z_grouped, lo, hi), woven(a_n1, lo, hi), woven(a_n2, lo, hi), ALU.subtract
+            )
+            quantize(z_codes, z_scales, z_grouped, lo, hi)
+
+        h_banks = []
+        for m in range(N // P):
+            bank = psum.tile([P, S], F32, name="bank%d" % m)
+            cols = slice(m * P, (m + 1) * P)
+            for s, (codes, scales) in enumerate(((z2_codes, z2_scales), (z_codes, z_scales))):
+                nc.tensor.matmul_mx(
+                    bank[:],
+                    lhsT=w_codes[s][:, cols].bitcast(FP8X4),
+                    lhsT_scale=w_scales[s][:, cols],
+                    rhs=codes[:].bitcast(FP8X4),
+                    rhs_scale=scales[:],
+                    start=(s == 0),
+                    stop=(s == 1),
+                )
+            h_banks.append(bank)
+
+        st_windows = []
+        for m in range(N // P):
+            h_window = result_window("h%d" % m)
+            nc.vector.tensor_copy(h_window[:, :S], h_banks[m][:])
+            h_n6 = keep.tile([P, S], F32, name="h_n6_%d" % m)
+            fetch(h_n6, h_window, n6_list)
+            st_window = result_window("st%d" % m)
+            nc.vector.tensor_tensor(st_window[:, :S], h_banks[m][:], h_n6[:], ALU.max)
+            st_windows.append(st_window)
+        for m in range(N // P):
+            st_n7 = keep.tile([P, S], F32, name="st_n7_%d" % m)
+            fetch(st_n7, st_windows[m], n7_list)
+            result = keep.tile([P, S], F32, name="result%d" % m)
+            nc.vector.scalar_tensor_tensor(result[:], h_banks[m][:], -0.5, st_n7[:], ALU.mult, ALU.add)
+            nc.sync.dma_start(out[m * P : (m + 1) * P, :], result[:])

@@ -45,39 +45,39 @@ def tile_picked_pqjgapkindahopb_none_p_kernel(
         d_byte_table = keep.tile([P, G], U8)
         x_byte_table = keep.tile([P, T], U8)
         planes = keep.tile([P, 2 * (H + S)], U8, align_bytes=64)
-        nc.vector.memset(d_byte_table[:].bitcast(I32), 0)
+        nc.gpsimd.memset(d_byte_table[:].bitcast(I32), 0)
         nc.vector.memset(x_byte_table[:].bitcast(I32), 0)
-        nc.gpsimd.memset(planes[:].bitcast(I32), 0)
-
-        k2_list = load_list("k2", k2)
-        k1_list = load_list("k1", k1)
-        two_list = load_list("two", two)
-        nc.sync.dma_start(d_byte_table[0:P:8, :].bitcast(I32), d_scales[0].bitcast(I32))
-        nc.sync.dma_start(x_byte_table[0:P:8, :].bitcast(I32), x_scales[0].bitcast(I32))
-        offs_list = load_list("offs", offs)
+        nc.vector.memset(planes[:].bitcast(I32), 0)
 
         tab_rows = tab.rearrange("(p t) c -> p t c", t=PACK)
         tab_tiles = [keep.tile([P, J], F32, name="tab%d" % t) for t in range(PACK)]
         x_word_table = keep.tile([P, T], U32)
         d_word_table = keep.tile([P, G], U32)
-        nc.sync.dma_start(tab_tiles[0][:], tab_rows[:, 0, :])
-        nc.sync.dma_start(x_word_table[:].bitcast(I32), x_words[0].rearrange("p n t -> p (n t)").bitcast(I32))
-        n3_list = load_list("n3", n3)
-        n4_list = load_list("n4", n4)
-        nc.sync.dma_start(d_word_table[:].bitcast(I32), d_words[0].rearrange("p n t -> p (n t)").bitcast(I32))
-        nc.sync.dma_start(tab_tiles[1][:], tab_rows[:, 1, :])
         gm_cols = keep.tile([P, PACK], F32)
         gn_cols = keep.tile([P, PACK], F32)
-        nc.sync.dma_start(gm_cols[:], gm.rearrange("(p t) o -> p (t o)", t=PACK))
-        nc.sync.dma_start(gn_cols[:], gn.rearrange("(p t) o -> p (t o)", t=PACK))
-        nc.sync.dma_start(tab_tiles[2][:], tab_rows[:, 2, :])
-        nc.sync.dma_start(tab_tiles[3][:], tab_rows[:, 3, :])
+
+        nc.sync.dma_start(d_byte_table[0:P:8, :].bitcast(I32), d_scales[0].bitcast(I32))
+        k2_list = load_list("k2", k2)
+        k1_list = load_list("k1", k1)
+        n4_list = load_list("n4", n4)
+        n3_list = load_list("n3", n3)
+        for t in range(PACK - 1):
+            nc.sync.dma_start(tab_tiles[t][:], tab_rows[:, t, :])
+        nc.sync.dma_start(x_byte_table[0:P:8, :].bitcast(I32), x_scales[0].bitcast(I32))
+        two_list = load_list("two", two)
+        offs_list = load_list("offs", offs)
+        nc.sync.dma_start(d_word_table[:].bitcast(I32), d_words[0].rearrange("p n t -> p (n t)").bitcast(I32))
         n5_list = load_list("n5", n5)
         n1_list = load_list("n1", n1)
         n2_list = load_list("n2", n2)
+        nc.sync.dma_start(x_word_table[:].bitcast(I32), x_words[0].rearrange("p n t -> p (n t)").bitcast(I32))
+        nc.sync.dma_start(tab_tiles[PACK - 1][:], tab_rows[:, PACK - 1, :])
+        n6_list = load_list("n6", n6)
+        n7_list = load_list("n7", n7)
+        nc.gpsimd.dma_start(gm_cols[:], gm.rearrange("(p t) o -> p (t o)", t=PACK))
+        nc.gpsimd.dma_start(gn_cols[:], gn.rearrange("(p t) o -> p (t o)", t=PACK))
 
-        staged = keep.tile([P, 2 * (H + S)], U8)
-        x_bytes = keep.tile([P, 2 * S], U8)
+        staged = keep.tile([P, 2 * (H + S)], U8, tag="w_raw1")
         for s, codes in enumerate((k2_list, k1_list)):
             d_bytes = keep.tile([P, H], U8, name="d_bytes%d" % s)
             nc.vector.tensor_copy(d_bytes[:], d_byte_table[:].indirect(codes[:]))
@@ -85,21 +85,20 @@ def tile_picked_pqjgapkindahopb_none_p_kernel(
                 staged[:, s * H : (s + 1) * H].rearrange("p (t c i) -> p c t i", t=PACK, i=16),
                 d_bytes[:].rearrange("p (c i t) -> p c t i", t=PACK, i=16),
             )
-        for s, tokens in enumerate((two_list, offs_list)):
-            nc.vector.tensor_copy(x_bytes[:, s * S : (s + 1) * S], x_byte_table[:].indirect(tokens[:]))
-        nc.vector.tensor_copy(staged[:, 2 * H :], x_bytes[:])
+        for tokens, tag, lo in ((two_list, "d_picked", 2 * H), (offs_list, "w_raw0", 2 * H + S)):
+            x_bytes = keep.tile([P, S], U8, name="x_bytes%d" % lo, tag=tag)
+            nc.vector.tensor_copy(x_bytes[:], x_byte_table[:].indirect(tokens[:]))
+            nc.vector.tensor_copy(staged[:, lo : lo + S], x_bytes[:])
         for q in range(4):
-            nc.scalar.dma_start(
+            nc.sync.dma_start(
                 planes[32 * q : 32 * q + 4, :].bitcast(I32), staged[32 * q : 32 * q + 32 : 8, :].bitcast(I32)
             )
 
         w_raw = []
         for s, w in enumerate((w2, w1)):
-            raw = keep.tile([P, PACK, N], F32, name="w_raw%d" % s)
+            raw = keep.tile([P, PACK, N], F32, name="w_raw%d" % s, tag="w_raw%d" % s)
             nc.sync.dma_start(raw[:], w.rearrange("(p t) n -> p t n", t=PACK))
             w_raw.append(raw)
-        n6_list = load_list("n6", n6)
-        n7_list = load_list("n7", n7)
 
         gm_16th = keep.tile([P, PACK], F32)
         gn_16th = keep.tile([P, PACK], F32)
@@ -116,14 +115,14 @@ def tile_picked_pqjgapkindahopb_none_p_kernel(
 
         def coded_product(s, codes, tokens):
             x_picked = keep.tile([P, S], U32, name="x_picked%d" % s, align_bytes=64)
-            d_picked = keep.tile([P, H], U32, name="d_picked%d" % s)
+            d_picked = keep.tile([P, H], U32, name="d_picked%d" % s, tag="d_picked")
             d_dealt = keep.tile([P, H], U32, name="d_dealt%d" % s, align_bytes=64)
-            nc.vector.tensor_copy(x_picked[:], x_word_table[:].indirect(tokens[:]))
             nc.vector.tensor_copy(d_picked[:], d_word_table[:].indirect(codes[:]))
             nc.vector.tensor_copy(
                 d_dealt[:].bitcast(I32).rearrange("p (t c i) -> p c t i", t=PACK, i=4),
                 d_picked[:].bitcast(I32).rearrange("p (c i t) -> p c t i", t=PACK, i=4),
             )
+            nc.vector.tensor_copy(x_picked[:], x_word_table[:].indirect(tokens[:]))
             banks = []
             for t in range(PACK):
                 bank = psum.tile([P, S], F32, name="bank%d" % (PACK * s + t))
@@ -161,12 +160,13 @@ def tile_picked_pqjgapkindahopb_none_p_kernel(
         a_windows = []
         for t in range(PACK):
             a_window = result_window("a%d" % t)
-            nc.vector.tensor_scalar(a_window[:, :S], a_banks[t][:], gn_16th[:, t : t + 1], None, ALU.mult)
+            nc.scalar.activation(a_window[:, :S], a_banks[t][:], COPY, scale=gn_16th[:, t : t + 1])
             a_windows.append(a_window)
 
         w_codes, w_scales = [], []
-        for s in range(2):
-            grouped = keep.tile([P, N, PACK], BF16, name="w_grouped%d" % s, align_bytes=64)
+
+        def quantize_weight(s):
+            grouped = keep.tile([P, N, PACK], BF16, name="w_grouped%d" % s, tag="grouped%d" % s, align_bytes=64)
             codes = keep.tile([P, N], U32, name="w_codes%d" % s, align_bytes=64)
             scales = keep.tile([P, N], U8, name="w_scales%d" % s, align_bytes=64)
             nc.vector.tensor_copy(weave_target(grouped, 0, N), woven(w_raw[s], 0, N))
@@ -174,22 +174,25 @@ def tile_picked_pqjgapkindahopb_none_p_kernel(
             w_codes.append(codes)
             w_scales.append(scales)
 
-        scaled = keep.tile([P, PACK, S], F32)
-        z2_grouped = keep.tile([P, S, PACK], BF16, align_bytes=64)
+        quantize_weight(0)
+        scaled = keep.tile([P, PACK, S], F32, tag="w_raw0")
+        z2_grouped = keep.tile([P, S, PACK], BF16, tag="grouped0", align_bytes=64)
         z2_codes = keep.tile([P, S], U32, align_bytes=64)
         z2_scales = keep.tile([P, S], U8, align_bytes=64)
         nc.vector.tensor_tensor(scaled[:], b_n5[:], tab_n3[:], ALU.mult)
         nc.vector.tensor_tensor(weave_target(z2_grouped, 0, S), woven(scaled, 0, S), woven(shift, 0, S), ALU.add)
         quantize(z2_codes, z2_scales, z2_grouped, 0, S)
 
+        quantize_weight(1)
         a_n1 = keep.tile([P, PACK, S], F32)
         a_n2 = keep.tile([P, PACK, S], F32)
-        z_grouped = keep.tile([P, S, PACK], BF16, align_bytes=64)
+        z_grouped = keep.tile([P, S, PACK], BF16, tag="grouped1", align_bytes=64)
         z_codes = keep.tile([P, S], U32, align_bytes=64)
         z_scales = keep.tile([P, S], U8, align_bytes=64)
+        for t in range(PACK):
+            fetch(a_n1[:, t, :], a_windows[t], n1_list)
         for lo, hi in ((0, S // 2), (S // 2, S)):
             for t in range(PACK):
-                fetch(a_n1[:, t, :], a_windows[t], n1_list, lo, hi)
                 fetch(a_n2[:, t, :], a_windows[t], n2_list, lo, hi)
             nc.vector.tensor_tensor(
                 weave_target(z_grouped, lo, hi), woven(a_n1, lo, hi), woven(a_n2, lo, hi), ALU.subtract

@@ -27,6 +27,7 @@ def tile_picked_pqjgapkindahopb_none_p_kernel(
     nc = tc.nc
     with ExitStack() as ctx:
         keep = ctx.enter_context(tc.tile_pool(name="keep", bufs=1))
+        shared = ctx.enter_context(tc.tile_pool(name="shared", bufs=1))
         psum = ctx.enter_context(tc.psum_pool(name="psum", bufs=1))
 
         def load_list(name, src):
@@ -44,10 +45,8 @@ def tile_picked_pqjgapkindahopb_none_p_kernel(
 
         d_byte_table = keep.tile([P, G], U8)
         x_byte_table = keep.tile([P, T], U8)
-        planes = keep.tile([P, 2 * (H + S)], U8, align_bytes=64)
         nc.gpsimd.memset(d_byte_table[:].bitcast(I32), 0)
         nc.vector.memset(x_byte_table[:].bitcast(I32), 0)
-        nc.vector.memset(planes[:].bitcast(I32), 0)
 
         tab_rows = tab.rearrange("(p t) c -> p t c", t=PACK)
         tab_tiles = [keep.tile([P, J], F32, name="tab%d" % t) for t in range(PACK)]
@@ -60,45 +59,44 @@ def tile_picked_pqjgapkindahopb_none_p_kernel(
         k2_list = load_list("k2", k2)
         k1_list = load_list("k1", k1)
         n4_list = load_list("n4", n4)
+        nc.sync.dma_start(tab_tiles[0][:], tab_rows[:, 0, :])
+        nc.sync.dma_start(tab_tiles[1][:], tab_rows[:, 1, :])
         n3_list = load_list("n3", n3)
-        for t in range(PACK - 1):
-            nc.sync.dma_start(tab_tiles[t][:], tab_rows[:, t, :])
         nc.sync.dma_start(x_byte_table[0:P:8, :].bitcast(I32), x_scales[0].bitcast(I32))
         two_list = load_list("two", two)
         offs_list = load_list("offs", offs)
-        nc.sync.dma_start(d_word_table[:].bitcast(I32), d_words[0].rearrange("p n t -> p (n t)").bitcast(I32))
+        nc.sync.dma_start(tab_tiles[2][:], tab_rows[:, 2, :])
+        nc.sync.dma_start(x_word_table[:].bitcast(I32), x_words[0].rearrange("p n t -> p (n t)").bitcast(I32))
         n5_list = load_list("n5", n5)
         n1_list = load_list("n1", n1)
         n2_list = load_list("n2", n2)
-        nc.sync.dma_start(x_word_table[:].bitcast(I32), x_words[0].rearrange("p n t -> p (n t)").bitcast(I32))
-        nc.sync.dma_start(tab_tiles[PACK - 1][:], tab_rows[:, PACK - 1, :])
+        nc.sync.dma_start(d_word_table[:].bitcast(I32), d_words[0].rearrange("p n t -> p (n t)").bitcast(I32))
+        nc.sync.dma_start(tab_tiles[3][:], tab_rows[:, 3, :])
         n6_list = load_list("n6", n6)
         n7_list = load_list("n7", n7)
         nc.gpsimd.dma_start(gm_cols[:], gm.rearrange("(p t) o -> p (t o)", t=PACK))
         nc.gpsimd.dma_start(gn_cols[:], gn.rearrange("(p t) o -> p (t o)", t=PACK))
 
-        staged = keep.tile([P, 2 * (H + S)], U8, tag="w_raw1")
+        planes = keep.tile([P, 2 * (H + S)], U8, align_bytes=64)
         for s, codes in enumerate((k2_list, k1_list)):
             d_bytes = keep.tile([P, H], U8, name="d_bytes%d" % s)
             nc.vector.tensor_copy(d_bytes[:], d_byte_table[:].indirect(codes[:]))
             nc.vector.tensor_copy(
-                staged[:, s * H : (s + 1) * H].rearrange("p (t c i) -> p c t i", t=PACK, i=16),
+                planes[:, s * H : (s + 1) * H].rearrange("p (t c i) -> p c t i", t=PACK, i=16),
                 d_bytes[:].rearrange("p (c i t) -> p c t i", t=PACK, i=16),
             )
-        for tokens, tag, lo in ((two_list, "d_picked", 2 * H), (offs_list, "w_raw0", 2 * H + S)):
-            x_bytes = keep.tile([P, S], U8, name="x_bytes%d" % lo, tag=tag)
-            nc.vector.tensor_copy(x_bytes[:], x_byte_table[:].indirect(tokens[:]))
-            nc.vector.tensor_copy(staged[:, lo : lo + S], x_bytes[:])
-        for q in range(4):
-            nc.sync.dma_start(
-                planes[32 * q : 32 * q + 4, :].bitcast(I32), staged[32 * q : 32 * q + 32 : 8, :].bitcast(I32)
-            )
+        x_bytes = shared.tile([P, 2 * S], U8, offset=4 * PACK * N - S)
+        for s, tokens in enumerate((two_list, offs_list)):
+            nc.vector.tensor_copy(x_bytes[:, s * S : (s + 1) * S], x_byte_table[:].indirect(tokens[:]))
+        nc.vector.tensor_copy(planes[:, 2 * H :], x_bytes[:])
+        for r in range(1, 4):
+            nc.sync.dma_start(planes[r:P:32, :].bitcast(I32), planes[8 * r : P : 32, :].bitcast(I32))
 
-        w_raw = []
-        for s, w in enumerate((w2, w1)):
-            raw = keep.tile([P, PACK, N], F32, name="w_raw%d" % s, tag="w_raw%d" % s)
+        w2_raw = shared.tile([P, PACK, N], F32, offset=0)
+        w1_raw = shared.tile([P, PACK, N], F32, offset=4 * PACK * N)
+        w_raw = [w2_raw, w1_raw]
+        for raw, w in zip(w_raw, (w2, w1)):
             nc.sync.dma_start(raw[:], w.rearrange("(p t) n -> p t n", t=PACK))
-            w_raw.append(raw)
 
         gm_16th = keep.tile([P, PACK], F32)
         gn_16th = keep.tile([P, PACK], F32)
@@ -111,7 +109,7 @@ def tile_picked_pqjgapkindahopb_none_p_kernel(
         for t in range(PACK):
             fetch(tab_n4[:, t, :], tab_tiles[t], n4_list)
             fetch(tab_n3[:, t, :], tab_tiles[t], n3_list)
-            nc.gpsimd.tensor_scalar(shift[:, t, :], tab_n4[:, t, :], gm_cols[:, t : t + 1], 0.0, ALU.mult, ALU.add)
+            nc.scalar.activation(shift[:, t, :], tab_n4[:, t, :], COPY, scale=gm_cols[:, t : t + 1])
 
         def coded_product(s, codes, tokens):
             x_picked = keep.tile([P, S], U32, name="x_picked%d" % s, align_bytes=64)
@@ -119,8 +117,8 @@ def tile_picked_pqjgapkindahopb_none_p_kernel(
             d_dealt = keep.tile([P, H], U32, name="d_dealt%d" % s, align_bytes=64)
             nc.vector.tensor_copy(d_picked[:], d_word_table[:].indirect(codes[:]))
             nc.vector.tensor_copy(
-                d_dealt[:].bitcast(I32).rearrange("p (t c i) -> p c t i", t=PACK, i=4),
-                d_picked[:].bitcast(I32).rearrange("p (c i t) -> p c t i", t=PACK, i=4),
+                d_dealt[:].bitcast(I32).rearrange("p (u e c i) -> p c u i e", u=2, e=2, i=4),
+                d_picked[:].bitcast(I32).rearrange("p (c i u e) -> p c u i e", u=2, e=2, i=4),
             )
             nc.vector.tensor_copy(x_picked[:], x_word_table[:].indirect(tokens[:]))
             banks = []
@@ -139,10 +137,10 @@ def tile_picked_pqjgapkindahopb_none_p_kernel(
             return banks
 
         def woven(planar, lo, hi):
-            return planar[:, :, lo:hi].rearrange("p t (c i) -> p c t i", i=4)
+            return planar[:, :, lo:hi].rearrange("p t (c i) -> p c t i", i=2)
 
         def weave_target(grouped, lo, hi):
-            return grouped[:, lo:hi, :].rearrange("p (c i) t -> p c t i", i=4)
+            return grouped[:, lo:hi, :].rearrange("p (c i) t -> p c t i", i=2)
 
         def quantize(codes, scales, grouped, lo, hi):
             nc.vector.quantize_mx(
@@ -175,11 +173,11 @@ def tile_picked_pqjgapkindahopb_none_p_kernel(
             w_scales.append(scales)
 
         quantize_weight(0)
-        scaled = keep.tile([P, PACK, S], F32, tag="w_raw0")
+        scaled = shared.tile([P, PACK, S], F32, offset=0)
+        nc.vector.tensor_tensor(scaled[:], b_n5[:], tab_n3[:], ALU.mult)
         z2_grouped = keep.tile([P, S, PACK], BF16, tag="grouped0", align_bytes=64)
         z2_codes = keep.tile([P, S], U32, align_bytes=64)
         z2_scales = keep.tile([P, S], U8, align_bytes=64)
-        nc.vector.tensor_tensor(scaled[:], b_n5[:], tab_n3[:], ALU.mult)
         nc.vector.tensor_tensor(weave_target(z2_grouped, 0, S), woven(scaled, 0, S), woven(shift, 0, S), ALU.add)
         quantize(z2_codes, z2_scales, z2_grouped, 0, S)
 
@@ -203,15 +201,16 @@ def tile_picked_pqjgapkindahopb_none_p_kernel(
         for m in range(N // P):
             bank = psum.tile([P, S], F32, name="bank%d" % m)
             cols = slice(m * P, (m + 1) * P)
-            for s, (codes, scales) in enumerate(((z2_codes, z2_scales), (z_codes, z_scales))):
+            passes = ((0, z2_codes, z2_scales, 0, S), (1, z_codes, z_scales, 0, S // 2), (1, z_codes, z_scales, S // 2, S))
+            for s, codes, scales, lo, hi in passes:
                 nc.tensor.matmul_mx(
-                    bank[:],
+                    bank[:, lo:hi],
                     lhsT=w_codes[s][:, cols].bitcast(FP8X4),
                     lhsT_scale=w_scales[s][:, cols],
-                    rhs=codes[:].bitcast(FP8X4),
-                    rhs_scale=scales[:],
+                    rhs=codes[:, lo:hi].bitcast(FP8X4),
+                    rhs_scale=scales[:, lo:hi],
                     start=(s == 0),
-                    stop=(s == 1),
+                    stop=(lo > 0),
                 )
             h_banks.append(bank)
 
@@ -226,7 +225,10 @@ def tile_picked_pqjgapkindahopb_none_p_kernel(
             st_windows.append(st_window)
         for m in range(N // P):
             st_n7 = keep.tile([P, S], F32, name="st_n7_%d" % m)
-            fetch(st_n7, st_windows[m], n7_list)
             result = keep.tile([P, S], F32, name="result%d" % m)
-            nc.vector.scalar_tensor_tensor(result[:], h_banks[m][:], -0.5, st_n7[:], ALU.mult, ALU.add)
-            nc.sync.dma_start(out[m * P : (m + 1) * P, :], result[:])
+            for lo, hi in ((0, S),) if m + 1 < N // P else ((0, S // 2), (S // 2, S)):
+                fetch(st_n7, st_windows[m], n7_list, lo, hi)
+                nc.vector.scalar_tensor_tensor(
+                    result[:, lo:hi], h_banks[m][:, lo:hi], -0.5, st_n7[:, lo:hi], ALU.mult, ALU.add
+                )
+                nc.sync.dma_start(out[m * P : (m + 1) * P, lo:hi], result[:, lo:hi])

from contextlib import ExitStack

import concourse.mybir as mybir

K, T, S, N, G, H, J = 512, 1024, 256, 512, 2048, 512, 512
FLOPS = 2 * (2 * K * H * S) + 2 * (2 * H * N * S)

F32 = mybir.dt.float32
BF16 = mybir.dt.bfloat16
I32 = mybir.dt.int32
U32 = mybir.dt.uint32
U16 = mybir.dt.uint16
U8 = mybir.dt.uint8
FP8X4 = mybir.dt.float8_e4m3fn_x4
ALU = mybir.AluOpType
COPY = mybir.ActivationFunctionType.Copy

P = 128
PACK = 4
SPARE = 8
LIST_ROWS = 16


def tile_picked_pqjgapkindahopb_none_p_kernel(
    tc, x_words, x_scales, d_words, d_scales, tab, gn, gm, w1, w2, offs, k1, two, k2, n1, n2, n3, n4, n5, n6, n7, out
):
    nc = tc.nc
    with ExitStack() as ctx:
        keep = ctx.enter_context(tc.tile_pool(name="keep", bufs=1))
        shared = ctx.enter_context(tc.tile_pool(name="shared", bufs=1))
        psum = ctx.enter_context(tc.psum_pool(name="psum", bufs=1))

        def load_list(name, src):
            tile = keep.tile(list(src.shape), U16, name="list_" + name)
            nc.sync.dma_start(tile[:], src)
            return tile

        def result_window(name):
            tile = keep.tile([P, S + SPARE], F32, name=name)
            nc.gpsimd.memset(tile[:, S:], 0.0)
            return tile

        def fetch(dst, window, places, lo=0, hi=S):
            nc.scalar.activation(dst[:, lo:hi], window[:].indirect(places[:, lo // LIST_ROWS : hi // LIST_ROWS]), COPY)

        d_byte_table = keep.tile([P, G], U8)
        x_byte_table = keep.tile([P, T], U8)
        nc.gpsimd.memset(d_byte_table[:].bitcast(I32), 0)
        nc.vector.memset(x_byte_table[:].bitcast(I32), 0)

        tab_rows = tab.rearrange("(p t) c -> p t c", t=PACK)
        tab_tiles = [keep.tile([P, J], F32, name="tab%d" % t) for t in range(PACK)]
        x_word_table = keep.tile([P, T], U32)
        d_word_table = keep.tile([P, G], U32)
        gm_cols = keep.tile([P, PACK], F32)
        gn_cols = keep.tile([P, PACK], F32)

        nc.sync.dma_start(d_byte_table[0:P:8, :].bitcast(I32), d_scales[0].bitcast(I32))
        k2_list = load_list("k2", k2)
        k1_list = load_list("k1", k1)
        n4_list = load_list("n4", n4)
        nc.sync.dma_start(tab_tiles[0][:], tab_rows[:, 0, :])
        nc.sync.dma_start(tab_tiles[1][:], tab_rows[:, 1, :])
        n3_list = load_list("n3", n3)
        nc.sync.dma_start(x_byte_table[0:P:8, :].bitcast(I32), x_scales[0].bitcast(I32))
        two_list = load_list("two", two)
        offs_list = load_list("offs", offs)
        nc.sync.dma_start(tab_tiles[2][:], tab_rows[:, 2, :])
        nc.sync.dma_start(x_word_table[:].bitcast(I32), x_words[0].rearrange("p n t -> p (n t)").bitcast(I32))
        n5_list = load_list("n5", n5)
        n1_list = load_list("n1", n1)
        n2_list = load_list("n2", n2)
        nc.sync.dma_start(d_word_table[:].bitcast(I32), d_words[0].rearrange("p n t -> p (n t)").bitcast(I32))
        nc.sync.dma_start(tab_tiles[3][:], tab_rows[:, 3, :])
        n6_list = load_list("n6", n6)
        n7_list = load_list("n7", n7)
        nc.gpsimd.dma_start(gm_cols[:], gm.rearrange("(p t) o -> p (t o)", t=PACK))
        nc.gpsimd.dma_start(gn_cols[:], gn.rearrange("(p t) o -> p (t o)", t=PACK))

        planes = keep.tile([P, 2 * (H + S)], U8, align_bytes=64)
        for s, codes in enumerate((k2_list, k1_list)):
            d_bytes = keep.tile([P, H], U8, name="d_bytes%d" % s)
            nc.vector.tensor_copy(d_bytes[:], d_byte_table[:].indirect(codes[:]))
            nc.vector.tensor_copy(
                planes[:, s * H : (s + 1) * H].rearrange("p (t c i) -> p c t i", t=PACK, i=16),
                d_bytes[:].rearrange("p (c i t) -> p c t i", t=PACK, i=16),
            )
        x_bytes = shared.tile([P, 2 * S], U8, offset=4 * PACK * N - S)
        for s, tokens in enumerate((two_list, offs_list)):
            nc.vector.tensor_copy(x_bytes[:, s * S : (s + 1) * S], x_byte_table[:].indirect(tokens[:]))
        nc.vector.tensor_copy(planes[:, 2 * H :], x_bytes[:])
        for r in range(1, 4):
            nc.sync.dma_start(planes[r:P:32, :].bitcast(I32), planes[8 * r : P : 32, :].bitcast(I32))

        w2_raw = shared.tile([P, PACK, N], F32, offset=0)
        w1_raw = shared.tile([P, PACK, N], F32, offset=4 * PACK * N)
        w_raw = [w2_raw, w1_raw]
        for raw, w in zip(w_raw, (w2, w1)):
            nc.sync.dma_start(raw[:], w.rearrange("(p t) n -> p t n", t=PACK))

        gm_16th = keep.tile([P, PACK], F32)
        gn_16th = keep.tile([P, PACK], F32)
        nc.gpsimd.tensor_scalar(gm_16th[:], gm_cols[:], 0.0625, 0.0, ALU.mult, ALU.add)
        nc.gpsimd.tensor_scalar(gn_16th[:], gn_cols[:], 0.0625, 0.0, ALU.mult, ALU.add)

        tab_n3 = keep.tile([P, PACK, S], F32)
        tab_n4 = keep.tile([P, PACK, S], F32)
        shift = keep.tile([P, PACK, S], F32)
        for t in range(PACK):
            fetch(tab_n4[:, t, :], tab_tiles[t], n4_list)
            fetch(tab_n3[:, t, :], tab_tiles[t], n3_list)
            nc.scalar.activation(shift[:, t, :], tab_n4[:, t, :], COPY, scale=gm_cols[:, t : t + 1])

        def coded_product(s, codes, tokens):
            x_picked = keep.tile([P, S], U32, name="x_picked%d" % s, align_bytes=64)
            d_picked = keep.tile([P, H], U32, name="d_picked%d" % s, tag="d_picked")
            d_dealt = keep.tile([P, H], U32, name="d_dealt%d" % s, align_bytes=64)
            nc.vector.tensor_copy(d_picked[:], d_word_table[:].indirect(codes[:]))
            nc.vector.tensor_copy(
                d_dealt[:].bitcast(I32).rearrange("p (u e c i) -> p c u i e", u=2, e=2, i=4),
                d_picked[:].bitcast(I32).rearrange("p (c i u e) -> p c u i e", u=2, e=2, i=4),
            )
            nc.vector.tensor_copy(x_picked[:], x_word_table[:].indirect(tokens[:]))
            banks = []
            for t in range(PACK):
                bank = psum.tile([P, S], F32, name="bank%d" % (PACK * s + t))
                nc.tensor.matmul_mx(
                    bank[:],
                    lhsT=d_dealt[:, t * P : (t + 1) * P].bitcast(FP8X4),
                    lhsT_scale=planes[:, s * H + t * P : s * H + (t + 1) * P],
                    rhs=x_picked[:].bitcast(FP8X4),
                    rhs_scale=planes[:, 2 * H + s * S : 2 * H + (s + 1) * S],
                    start=True,
                    stop=True,
                )
                banks.append(bank)
            return banks

        def woven(planar, lo, hi):
            return planar[:, :, lo:hi].rearrange("p t (c i) -> p c t i", i=2)

        def weave_target(grouped, lo, hi):
            return grouped[:, lo:hi, :].rearrange("p (c i) t -> p c t i", i=2)

        def quantize(codes, scales, grouped, lo, hi):
            nc.vector.quantize_mx(
                codes[:, lo:hi].bitcast(FP8X4), scales[:, lo:hi], grouped[:, lo:hi, :].rearrange("p c t -> p (c t)")
            )

        b_banks = coded_product(0, k2_list, two_list)
        a_banks = coded_product(1, k1_list, offs_list)
        b_n5 = keep.tile([P, PACK, S], F32)
        for t in range(PACK):
            b_window = result_window("b%d" % t)
            nc.scalar.activation(b_window[:, :S], b_banks[t][:], COPY, scale=gm_16th[:, t : t + 1])
            fetch(b_n5[:, t, :], b_window, n5_list)

        a_windows = []
        for t in range(PACK):
            a_window = result_window("a%d" % t)
            nc.scalar.activation(a_window[:, :S], a_banks[t][:], COPY, scale=gn_16th[:, t : t + 1])
            a_windows.append(a_window)

        w_codes, w_scales = [], []

        def quantize_weight(s):
            grouped = keep.tile([P, N, PACK], BF16, name="w_grouped%d" % s, tag="grouped%d" % s, align_bytes=64)
            codes = keep.tile([P, N], U32, name="w_codes%d" % s, align_bytes=64)
            scales = keep.tile([P, N], U8, name="w_scales%d" % s, align_bytes=64)
            nc.vector.tensor_copy(weave_target(grouped, 0, N), woven(w_raw[s], 0, N))
            quantize(codes, scales, grouped, 0, N)
            w_codes.append(codes)
            w_scales.append(scales)

        quantize_weight(0)
        scaled = shared.tile([P, PACK, S], F32, offset=0)
        nc.vector.tensor_tensor(scaled[:], b_n5[:], tab_n3[:], ALU.mult)
        z2_grouped = keep.tile([P, S, PACK], BF16, tag="grouped0", align_bytes=64)
        z2_codes = keep.tile([P, S], U32, align_bytes=64)
        z2_scales = keep.tile([P, S], U8, align_bytes=64)
        nc.vector.tensor_tensor(weave_target(z2_grouped, 0, S), woven(scaled, 0, S), woven(shift, 0, S), ALU.add)
        quantize(z2_codes, z2_scales, z2_grouped, 0, S)

        quantize_weight(1)
        a_n1 = keep.tile([P, PACK, S], F32)
        a_n2 = keep.tile([P, PACK, S], F32)
        z_grouped = keep.tile([P, S, PACK], BF16, tag="grouped1", align_bytes=64)
        z_codes = keep.tile([P, S], U32, align_bytes=64)
        z_scales = keep.tile([P, S], U8, align_bytes=64)
        for t in range(PACK):
            fetch(a_n1[:, t, :], a_windows[t], n1_list)
        for lo, hi in ((0, S // 2), (S // 2, S)):
            for t in range(PACK):
                fetch(a_n2[:, t, :], a_windows[t], n2_list, lo, hi)
            nc.vector.tensor_tensor(
                weave_target(z_grouped, lo, hi), woven(a_n1, lo, hi), woven(a_n2, lo, hi), ALU.subtract
            )
            quantize(z_codes, z_scales, z_grouped, lo, hi)

        h_banks = []
        for m in range(N // P):
            bank = psum.tile([P, S], F32, name="bank%d" % m)
            cols = slice(m * P, (m + 1) * P)
            passes = ((0, z2_codes, z2_scales, 0, S), (1, z_codes, z_scales, 0, S // 2), (1, z_codes, z_scales, S // 2, S))
            for s, codes, scales, lo, hi in passes:
                nc.tensor.matmul_mx(
                    bank[:, lo:hi],
                    lhsT=w_codes[s][:, cols].bitcast(FP8X4),
                    lhsT_scale=w_scales[s][:, cols],
                    rhs=codes[:, lo:hi].bitcast(FP8X4),
                    rhs_scale=scales[:, lo:hi],
                    start=(s == 0),
                    stop=(lo > 0),
                )
            h_banks.append(bank)

        st_windows = []
        for m in range(N // P):
            h_window = result_window("h%d" % m)
            nc.vector.tensor_copy(h_window[:, :S], h_banks[m][:])
            h_n6 = keep.tile([P, S], F32, name="h_n6_%d" % m)
            fetch(h_n6, h_window, n6_list)
            st_window = result_window("st%d" % m)
            nc.vector.tensor_tensor(st_window[:, :S], h_banks[m][:], h_n6[:], ALU.max)
            st_windows.append(st_window)
        for m in range(N // P):
            st_n7 = keep.tile([P, S], F32, name="st_n7_%d" % m)
            result = keep.tile([P, S], F32, name="result%d" % m)
            for lo, hi in ((0, S),) if m + 1 < N // P else ((0, S // 2), (S // 2, S)):
                fetch(st_n7, st_windows[m], n7_list, lo, hi)
                nc.vector.scalar_tensor_tensor(
                    result[:, lo:hi], h_banks[m][:, lo:hi], -0.5, st_n7[:, lo:hi], ALU.mult, ALU.add
                )
                nc.sync.dma_start(out[m * P : (m + 1) * P, lo:hi], result[:, lo:hi])
